import numpy as np, ml_dtypes
CORES = [29,2,10,18,34,42,50,58,66,74,82,90,98,106,114,122]
N = 16
ROOT = 0
def setup_inputs(rng):
    return {"x": rng.standard_normal((N, 128, 2048), dtype=np.float32).astype(ml_dtypes.bfloat16)}
def reference(x):
    return {"y": np.broadcast_to(x[ROOT], x.shape)}

@@ -1,0 +1,224 @@
+import concourse.bass as bass
+import comms_topo
+
+VARIANT = "hy"
+
+ROOT = 29
+RANKS = [8 * ch + 2 for ch in range(16) if ch != 3]
+ODD = [1, 5, 7, 9, 11, 13, 15]
+EVEN = [0, 2, 4, 6, 8, 10, 12, 14]
+HELP = [30, 26, 31, 27]
+
+
+def eng(lo, n):
+    return ((1 << n) - 1) << lo
+
+
+def pow2_floor(v):
+    n = 1
+    while 2 * n <= v:
+        n *= 2
+    return n
+
+
+def group_of(p, bounds):
+    j = 0
+    while p >= bounds[j + 1]:
+        j += 1
+    return "g%d" % j
+
+
+def finish(prog, bounds):
+    for r in RANKS:
+        for j in range(len(bounds) - 1):
+            prog[r].append(("W", "g%d" % j))
+            prog[r].append(("ST", bounds[j], bounds[j + 1]))
+        prog[r].append(("W", "st"))
+    for c in prog:
+        if any(op[0] == "S" for op in prog[c]):
+            prog[c].append(("W", "sent"))
+    tot = {}
+    for c in prog:
+        for op in prog[c]:
+            if op[0] == "S":
+                for (p, dsts, mask, sem) in op[1]:
+                    n = bin(mask).count("1")
+                    tot[(c, "sent")] = tot.get((c, "sent"), 0) + n
+                    for d in dsts:
+                        tot[(d, sem)] = tot.get((d, sem), 0) + n
+            elif op[0] == "LD":
+                tot[(c, op[3])] = tot.get((c, op[3]), 0) + 16
+            elif op[0] in ("ST", "XY"):
+                tot[(c, "st")] = tot.get((c, "st"), 0) + 16
+    return prog, tot
+
+
+def resend(prog, core, pieces, bounds, split, sem="pc"):
+    dsts = [r for r in RANKS if r > core] + [r for r in RANKS if r < core]
+    n = 8 // (len(pieces) * split)
+    trs = []
+    for i, p in enumerate(pieces):
+        for s in range(split):
+            part = dsts[s::split]
+            trs.append((p, part, eng((i * split + s) * n, n), group_of(p, bounds)))
+    prog[core].append(("W", sem))
+    prog[core].append(("S", trs))
+
+
+def build_hy(nt=4, order="efirst", split=1, chold=None, merge_tail=False):
+    types = [2, 6, 3, 7][:nt]
+    npc = 16 * nt
+    ncol = 2048 // npc
+    chold = chold or HELP[:nt]
+    per = 2 * nt
+    e_all = [("E", e) for e in range(8 * nt)]
+    o_all = [("O", k) for k in range(7 * nt)]
+    c_all = [("C", i) for i in range(nt)]
+    calls = []
+    if order == "efirst":
+        for a in range(0, 8 * nt, 16):
+            calls.append(e_all[a:a + 16])
+        calls.append(c_all + o_all[0:8])
+        for a in range(8, 7 * nt, 8):
+            calls.append(o_all[a:a + 8])
+    elif order == "mix":
+        calls = [e_all[0:16], e_all[16:24] + o_all[0:8], e_all[24:32] + o_all[8:16], c_all + o_all[16:24],
+                 o_all[24:28]]
+    elif order == "ofirst":
+        calls = [e_all[0:8] + o_all[0:8], e_all[8:16] + o_all[8:16], e_all[16:24] + o_all[16:24],
+                 e_all[24:32] + o_all[24:28] + c_all]
+    num, p = {}, 0
+    cuts = [0]
+    for call in calls:
+        for it in call:
+            num[it] = p
+            p += 1
+        cuts.append(p)
+    bounds = list(cuts)
+    if merge_tail:
+        bounds = bounds[:-2] + bounds[-1:]
+    prog = {c: [] for c in range(128)}
+    root = prog[ROOT]
+    lcuts = list(range(0, npc + 1, npc // 4))
+    for i in range(4):
+        root.append(("LD", lcuts[i], lcuts[i + 1], "ld%d" % i))
+    e_holder = [8 * EVEN[e % 8] + types[e // 8] for e in range(8 * nt)]
+    o_holder = [8 * ODD[k % 7] + types[k // 7] for k in range(7 * nt)]
+    for h in range(4):
+        w = 8 // per
+        prog[HELP[h]].append(("W", "he"))
+        prog[HELP[h]].append(("S", [(num[("E", h * per + j)], [e_holder[h * per + j]], eng(j * w, w), "pc")
+                                    for j in range(per)]))
+    for e in range(8 * nt):
+        resend(prog, e_holder[e], [num[("E", e)]], bounds, split)
+    for k in range(7 * nt):
+        resend(prog, o_holder[k], [num[("O", k)]], bounds, split)
+    for c in sorted(set(chold)):
+        mine = [num[("C", i)] for i in range(nt) if chold[i] == c]
+        resend(prog, c, mine, bounds, max(1, split // len(mine)))
+    loaded = 0
+    for ci, call in enumerate(calls):
+        while lcuts[loaded] < cuts[ci + 1]:
+            root.append(("W", "ld%d" % loaded))
+            loaded += 1
+        off = [it for it in call if it[0] == "O"]
+        on = [it for it in call if it[0] != "O"]
+        trs = []
+        wo = pow2_floor(8 // len(off)) if off else 0
+        for i, it in enumerate(off):
+            trs.append((num[it], [o_holder[it[1]]], eng(i * wo, wo), "pc"))
+        base = len(off) * wo
+        if on:
+            wi = pow2_floor((16 - base) // len(on))
+            base = 16 - wi * len(on)
+            for i, it in enumerate(on):
+                if it[0] == "E":
+                    trs.append((num[it], [HELP[it[1] // per]], eng(base + i * wi, wi), "he"))
+                else:
+                    trs.append((num[it], [chold[it[1]]], eng(base + i * wi, wi), "pc"))
+        root.append(("S", trs))
+    root.append(("XY",))
+    root.append(("W", "st"))
+    return (ncol, npc) + finish(prog, bounds)
+
+
+def build_d2(split=1):
+    types = [2, 6, 3, 7]
+    ncol, npc = 64, 32
+    bounds = [0, 4, 12, 20, 28, 32]
+    prog = {c: [] for c in range(128)}
+    root = prog[ROOT]
+    cuts = [0, 12, 20, 28, 32]
+    for i in range(4):
+        root.append(("LD", cuts[i], cuts[i + 1], "ld%d" % i))
+    even_r = [r for r in RANKS if (r // 8) % 2 == 0]
+    odd_r = [r for r in RANKS if (r // 8) % 2 == 1]
+    side = [24, 25, 24, 25]
+    first = [(i, [HELP[i], side[i]], eng(8 + 2 * i, 2), "pc") for i in range(4)]
+    for i in range(4):
+        prog[HELP[i]].append(("W", "pc"))
+        n = 8 // split
+        prog[HELP[i]].append(("S", [(i, even_r[s::split], eng(s * n, n), "g0") for s in range(split)]))
+    for s in range(2):
+        prog[24 + s].append(("W", "pc"))
+        sp = max(1, split // 2)
+        n = 4 // sp
+        prog[24 + s].append(("S", [(s + 2 * a, odd_r[b::sp], eng((a * sp + b) * n, n), "g0")
+                                   for a in range(2) for b in range(sp)]))
+    holder = [8 * ODD[k % 7] + types[k // 7] for k in range(28)]
+    for k in range(28):
+        resend(prog, holder[k], [4 + k], bounds, split)
+    for call in range(4):
+        root.append(("W", "ld%d" % call))
+        if call < 3:
+            tr = [(4 + k, [holder[k]], 1 << (k - 8 * call), "pc") for k in range(8 * call, 8 * call + 8)]
+        else:
+            tr = [(4 + k, [holder[k]], eng(2 * (k - 24), 2), "pc") for k in range(24, 28)]
+        root.append(("S", (first if call == 0 else []) + tr))
+    root.append(("XY",))
+    root.append(("W", "st"))
+    return (ncol, npc) + finish(prog, bounds)
+
+
+BUILD = {
+    "hy": lambda: build_hy(),
+    "hy_s8": lambda: build_hy(split=8),
+    "hy_s4": lambda: build_hy(split=4),
+    "hy_mix": lambda: build_hy(order="mix"),
+    "hy_mix_s8": lambda: build_hy(order="mix", split=8),
+    "hy_of_s8": lambda: build_hy(order="ofirst", split=8),
+    "hy_c1_s8": lambda: build_hy(split=8, chold=[26, 27, 26, 27]),
+    "hy16": lambda: build_hy(nt=2),
+    "hy16_s8": lambda: build_hy(nt=2, split=8),
+    "d2": lambda: build_d2(),
+    "d2_s8": lambda: build_d2(split=8),
+}
+NCOL, NP, PROG, TOTAL = BUILD[VARIANT]()
+
+SCRATCH = {
+    "buf": ("dram", [NP, 128, NCOL], "bfloat16"),
+}
+SEMAPHORES = ["ld0", "ld1", "ld2", "ld3", "st", "sent", "he", "pc", "g0", "g1", "g2", "g3", "g4", "g5", "g6", "g7"]
+
+
+def rank_program(g, core, T, topo):
+    sems = {"ld0": T.sem.ld0, "ld1": T.sem.ld1, "ld2": T.sem.ld2, "ld3": T.sem.ld3, "st": T.sem.st,
+            "sent": T.sem.sent, "he": T.sem.he, "pc": T.sem.pc, "g0": T.sem.g0, "g1": T.sem.g1, "g2": T.sem.g2,
+            "g3": T.sem.g3, "g4": T.sem.g4, "g5": T.sem.g5, "g6": T.sem.g6, "g7": T.sem.g7}
+    rows = NCOL // 16
+    for op in PROG[core]:
+        if op[0] == "W":
+            g.wait_ge(sems[op[1]], TOTAL[(core, op[1])])
+        elif op[0] == "LD":
+            g.dma_start(T.buf[op[1]:op[2]], T.x[op[1] * rows:op[2] * rows, :]).then_inc(sems[op[3]], 16)
+        elif op[0] == "ST":
+            g.dma_start(T.y[op[1] * rows:op[2] * rows, :], T.buf[op[1]:op[2]]).then_inc(sems["st"], 16)
+        elif op[0] == "XY":
+            g.dma_start(T.y[:, :], T.x[:, :]).then_inc(sems["st"], 16)
+        else:
+            trs = []
+            for (p, dsts, mask, sem) in op[1]:
+                ids = [bass.DstId(rid=topo.addr(d)[0], pnc=topo.addr(d)[1]) for d in dsts]
+                trs.append(bass.RemoteDMATransfer(dst_ids=ids, dma_engine_mask=mask, remote_sem=sems[sem],
+                                                  srcs=[T.buf[p]], dsts=[T.buf[p] for d in dsts], alu_op=0))
+            g.remote_dma_fused(trs, local_sem=sems["sent"])

@@ -1,7 +1,7 @@
 import concourse.bass as bass
 import comms_topo
 
-VARIANT = "hy"
+VARIANT = "d2"
 
 ROOT = 29
 RANKS = [8 * ch + 2 for ch in range(16) if ch != 3]
@@ -84,9 +84,6 @@ def build_hy(nt=4, order="efirst", split=1, chold=None, merge_tail=False):
     elif order == "mix":
         calls = [e_all[0:16], e_all[16:24] + o_all[0:8], e_all[24:32] + o_all[8:16], c_all + o_all[16:24],
                  o_all[24:28]]
-    elif order == "ofirst":
-        calls = [e_all[0:8] + o_all[0:8], e_all[8:16] + o_all[8:16], e_all[16:24] + o_all[16:24],
-                 e_all[24:32] + o_all[24:28] + c_all]
     num, p = {}, 0
     cuts = [0]
     for call in calls:
@@ -186,7 +183,6 @@ BUILD = {
     "hy_s4": lambda: build_hy(split=4),
     "hy_mix": lambda: build_hy(order="mix"),
     "hy_mix_s8": lambda: build_hy(order="mix", split=8),
-    "hy_of_s8": lambda: build_hy(order="ofirst", split=8),
     "hy_c1_s8": lambda: build_hy(split=8, chold=[26, 27, 26, 27]),
     "hy16": lambda: build_hy(nt=2),
     "hy16_s8": lambda: build_hy(nt=2, split=8),

@@ -1,38 +1,26 @@
 import concourse.bass as bass
 import comms_topo
 
-VARIANT = "d2"
+FAR = 4
 
 ROOT = 29
 RANKS = [8 * ch + 2 for ch in range(16) if ch != 3]
+EVEN_R = [r for r in RANKS if (r // 8) % 2 == 0]
+ODD_R = [r for r in RANKS if (r // 8) % 2 == 1]
 ODD = [1, 5, 7, 9, 11, 13, 15]
-EVEN = [0, 2, 4, 6, 8, 10, 12, 14]
 HELP = [30, 26, 31, 27]
+SIDE = [24, 25, 24, 25]
 
 
 def eng(lo, n):
     return ((1 << n) - 1) << lo
 
 
-def pow2_floor(v):
-    n = 1
-    while 2 * n <= v:
-        n *= 2
-    return n
-
-
-def group_of(p, bounds):
-    j = 0
-    while p >= bounds[j + 1]:
-        j += 1
-    return "g%d" % j
-
-
-def finish(prog, bounds):
+def finish(prog, groups):
     for r in RANKS:
-        for j in range(len(bounds) - 1):
+        for j, (b, lo, hi) in enumerate(groups):
             prog[r].append(("W", "g%d" % j))
-            prog[r].append(("ST", bounds[j], bounds[j + 1]))
+            prog[r].append(("ST", b, lo, hi))
         prog[r].append(("W", "st"))
     for c in prog:
         if any(op[0] == "S" for op in prog[c]):
@@ -47,174 +35,93 @@ def finish(prog, bounds):
                     for d in dsts:
                         tot[(d, sem)] = tot.get((d, sem), 0) + n
             elif op[0] == "LD":
-                tot[(c, op[3])] = tot.get((c, op[3]), 0) + 16
+                tot[(c, op[4])] = tot.get((c, op[4]), 0) + 16
             elif op[0] in ("ST", "XY"):
                 tot[(c, "st")] = tot.get((c, "st"), 0) + 16
     return prog, tot
 
 
-def resend(prog, core, pieces, bounds, split, sem="pc"):
-    dsts = [r for r in RANKS if r > core] + [r for r in RANKS if r < core]
-    n = 8 // (len(pieces) * split)
-    trs = []
-    for i, p in enumerate(pieces):
-        for s in range(split):
-            part = dsts[s::split]
-            trs.append((p, part, eng((i * split + s) * n, n), group_of(p, bounds)))
-    prog[core].append(("W", sem))
-    prog[core].append(("S", trs))
+def resend(core, piece, gname, far):
+    if not far:
+        return [(piece, [r for r in RANKS if r > core] + [r for r in RANKS if r < core], 0xFF, gname)]
+    ev = [r for r in EVEN_R if r > core] + [r for r in EVEN_R if r < core]
+    od = [r for r in ODD_R if r > core] + [r for r in ODD_R if r < core]
+    w = 8 // far
+    return [(piece, ev[s::far] + od[s::far], eng(s * w, w), gname) for s in range(far)]
 
 
-def build_hy(nt=4, order="efirst", split=1, chold=None, merge_tail=False):
-    types = [2, 6, 3, 7][:nt]
-    npc = 16 * nt
-    ncol = 2048 // npc
-    chold = chold or HELP[:nt]
-    per = 2 * nt
-    e_all = [("E", e) for e in range(8 * nt)]
-    o_all = [("O", k) for k in range(7 * nt)]
-    c_all = [("C", i) for i in range(nt)]
-    calls = []
-    if order == "efirst":
-        for a in range(0, 8 * nt, 16):
-            calls.append(e_all[a:a + 16])
-        calls.append(c_all + o_all[0:8])
-        for a in range(8, 7 * nt, 8):
-            calls.append(o_all[a:a + 8])
-    elif order == "mix":
-        calls = [e_all[0:16], e_all[16:24] + o_all[0:8], e_all[24:32] + o_all[8:16], c_all + o_all[16:24],
-                 o_all[24:28]]
-    num, p = {}, 0
-    cuts = [0]
-    for call in calls:
-        for it in call:
-            num[it] = p
-            p += 1
-        cuts.append(p)
-    bounds = list(cuts)
-    if merge_tail:
-        bounds = bounds[:-2] + bounds[-1:]
+def build(far):
+    counts_o = [8, 8, 8, 4]
+    counts = [12, 8, 8, 4]
     prog = {c: [] for c in range(128)}
     root = prog[ROOT]
-    lcuts = list(range(0, npc + 1, npc // 4))
+    for q in range(4):
+        root.append(("LD", q, 0, counts[q], "ld%d" % q))
+    groups = [(0, 0, 4), (0, 4, 12), (1, 0, 8), (2, 0, 8), (3, 0, 4)]
+    first = [((0, i), [HELP[i], SIDE[i]], eng(8 + 2 * i, 2), "pc") for i in range(4)]
+    n = max(1, far)
+    m = max(1, far // 2)
     for i in range(4):
-        root.append(("LD", lcuts[i], lcuts[i + 1], "ld%d" % i))
-    e_holder = [8 * EVEN[e % 8] + types[e // 8] for e in range(8 * nt)]
-    o_holder = [8 * ODD[k % 7] + types[k // 7] for k in range(7 * nt)]
-    for h in range(4):
-        w = 8 // per
-        prog[HELP[h]].append(("W", "he"))
-        prog[HELP[h]].append(("S", [(num[("E", h * per + j)], [e_holder[h * per + j]], eng(j * w, w), "pc")
-                                    for j in range(per)]))
-    for e in range(8 * nt):
-        resend(prog, e_holder[e], [num[("E", e)]], bounds, split)
-    for k in range(7 * nt):
-        resend(prog, o_holder[k], [num[("O", k)]], bounds, split)
-    for c in sorted(set(chold)):
-        mine = [num[("C", i)] for i in range(nt) if chold[i] == c]
-        resend(prog, c, mine, bounds, max(1, split // len(mine)))
-    loaded = 0
-    for ci, call in enumerate(calls):
-        while lcuts[loaded] < cuts[ci + 1]:
-            root.append(("W", "ld%d" % loaded))
-            loaded += 1
-        off = [it for it in call if it[0] == "O"]
-        on = [it for it in call if it[0] != "O"]
-        trs = []
-        wo = pow2_floor(8 // len(off)) if off else 0
-        for i, it in enumerate(off):
-            trs.append((num[it], [o_holder[it[1]]], eng(i * wo, wo), "pc"))
-        base = len(off) * wo
-        if on:
-            wi = pow2_floor((16 - base) // len(on))
-            base = 16 - wi * len(on)
-            for i, it in enumerate(on):
-                if it[0] == "E":
-                    trs.append((num[it], [HELP[it[1] // per]], eng(base + i * wi, wi), "he"))
-                else:
-                    trs.append((num[it], [chold[it[1]]], eng(base + i * wi, wi), "pc"))
+        prog[HELP[i]].append(("W", "pc"))
+        prog[HELP[i]].append(("S", [((0, i), EVEN_R[s::n], eng(s * (8 // n), 8 // n), "g0") for s in range(n)]))
+    for s in range(2):
+        prog[24 + s].append(("W", "pc"))
+        prog[24 + s].append(("S", [((0, s + 2 * a), ODD_R[b::m], eng((a * m + b) * (4 // m), 4 // m), "g0")
+                                   for a in range(2) for b in range(m)]))
+    k = 0
+    for q in range(4):
+        base = 4 if q == 0 else 0
+        wo = 8 // counts_o[q]
+        trs = list(first) if q == 0 else []
+        for i in range(counts_o[q]):
+            core = 8 * ODD[k % 7] + [2, 6, 3, 7][k // 7]
+            k += 1
+            trs.append(((q, base + i), [core], eng(i * wo, wo), "pc"))
+            prog[core].append(("W", "pc"))
+            prog[core].append(("S", resend(core, (q, base + i), "g%d" % (q + 1), far)))
+        root.append(("W", "ld%d" % q))
         root.append(("S", trs))
     root.append(("XY",))
     root.append(("W", "st"))
-    return (ncol, npc) + finish(prog, bounds)
+    return ([64, 64, 64, 64], counts) + finish(prog, groups)
 
 
-def build_d2(split=1):
-    types = [2, 6, 3, 7]
-    ncol, npc = 64, 32
-    bounds = [0, 4, 12, 20, 28, 32]
-    prog = {c: [] for c in range(128)}
-    root = prog[ROOT]
-    cuts = [0, 12, 20, 28, 32]
-    for i in range(4):
-        root.append(("LD", cuts[i], cuts[i + 1], "ld%d" % i))
-    even_r = [r for r in RANKS if (r // 8) % 2 == 0]
-    odd_r = [r for r in RANKS if (r // 8) % 2 == 1]
-    side = [24, 25, 24, 25]
-    first = [(i, [HELP[i], side[i]], eng(8 + 2 * i, 2), "pc") for i in range(4)]
-    for i in range(4):
-        prog[HELP[i]].append(("W", "pc"))
-        n = 8 // split
-        prog[HELP[i]].append(("S", [(i, even_r[s::split], eng(s * n, n), "g0") for s in range(split)]))
-    for s in range(2):
-        prog[24 + s].append(("W", "pc"))
-        sp = max(1, split // 2)
-        n = 4 // sp
-        prog[24 + s].append(("S", [(s + 2 * a, odd_r[b::sp], eng((a * sp + b) * n, n), "g0")
-                                   for a in range(2) for b in range(sp)]))
-    holder = [8 * ODD[k % 7] + types[k // 7] for k in range(28)]
-    for k in range(28):
-        resend(prog, holder[k], [4 + k], bounds, split)
-    for call in range(4):
-        root.append(("W", "ld%d" % call))
-        if call < 3:
-            tr = [(4 + k, [holder[k]], 1 << (k - 8 * call), "pc") for k in range(8 * call, 8 * call + 8)]
-        else:
-            tr = [(4 + k, [holder[k]], eng(2 * (k - 24), 2), "pc") for k in range(24, 28)]
-        root.append(("S", (first if call == 0 else []) + tr))
-    root.append(("XY",))
-    root.append(("W", "st"))
-    return (ncol, npc) + finish(prog, bounds)
-
-
-BUILD = {
-    "hy": lambda: build_hy(),
-    "hy_s8": lambda: build_hy(split=8),
-    "hy_s4": lambda: build_hy(split=4),
-    "hy_mix": lambda: build_hy(order="mix"),
-    "hy_mix_s8": lambda: build_hy(order="mix", split=8),
-    "hy_c1_s8": lambda: build_hy(split=8, chold=[26, 27, 26, 27]),
-    "hy16": lambda: build_hy(nt=2),
-    "hy16_s8": lambda: build_hy(nt=2, split=8),
-    "d2": lambda: build_d2(),
-    "d2_s8": lambda: build_d2(split=8),
-}
-NCOL, NP, PROG, TOTAL = BUILD[VARIANT]()
+NCOLS, COUNTS, PROG, TOTAL = build(FAR)
+ROW0 = [0]
+for q in range(4):
+    ROW0.append(ROW0[q] + COUNTS[q] * NCOLS[q] // 16)
 
 SCRATCH = {
-    "buf": ("dram", [NP, 128, NCOL], "bfloat16"),
+    "bufa": ("dram", [COUNTS[0], 128, NCOLS[0]], "bfloat16"),
+    "bufb": ("dram", [COUNTS[1], 128, NCOLS[1]], "bfloat16"),
+    "bufc": ("dram", [COUNTS[2], 128, NCOLS[2]], "bfloat16"),
+    "bufd": ("dram", [COUNTS[3], 128, NCOLS[3]], "bfloat16"),
 }
-SEMAPHORES = ["ld0", "ld1", "ld2", "ld3", "st", "sent", "he", "pc", "g0", "g1", "g2", "g3", "g4", "g5", "g6", "g7"]
+SEMAPHORES = ["ld0", "ld1", "ld2", "ld3", "st", "sent", "pc", "g0", "g1", "g2", "g3", "g4"]
 
 
 def rank_program(g, core, T, topo):
     sems = {"ld0": T.sem.ld0, "ld1": T.sem.ld1, "ld2": T.sem.ld2, "ld3": T.sem.ld3, "st": T.sem.st,
-            "sent": T.sem.sent, "he": T.sem.he, "pc": T.sem.pc, "g0": T.sem.g0, "g1": T.sem.g1, "g2": T.sem.g2,
-            "g3": T.sem.g3, "g4": T.sem.g4, "g5": T.sem.g5, "g6": T.sem.g6, "g7": T.sem.g7}
-    rows = NCOL // 16
+            "sent": T.sem.sent, "pc": T.sem.pc, "g0": T.sem.g0, "g1": T.sem.g1, "g2": T.sem.g2,
+            "g3": T.sem.g3, "g4": T.sem.g4}
+    bufs = [T.bufa, T.bufb, T.bufc, T.bufd]
     for op in PROG[core]:
         if op[0] == "W":
             g.wait_ge(sems[op[1]], TOTAL[(core, op[1])])
-        elif op[0] == "LD":
-            g.dma_start(T.buf[op[1]:op[2]], T.x[op[1] * rows:op[2] * rows, :]).then_inc(sems[op[3]], 16)
-        elif op[0] == "ST":
-            g.dma_start(T.y[op[1] * rows:op[2] * rows, :], T.buf[op[1]:op[2]]).then_inc(sems["st"], 16)
+        elif op[0] in ("LD", "ST"):
+            b, lo, hi = op[1], op[2], op[3]
+            r0 = ROW0[b] + lo * NCOLS[b] // 16
+            r1 = ROW0[b] + hi * NCOLS[b] // 16
+            if op[0] == "LD":
+                g.dma_start(bufs[b][lo:hi], T.x[r0:r1, :]).then_inc(sems[op[4]], 16)
+            else:
+                g.dma_start(T.y[r0:r1, :], bufs[b][lo:hi]).then_inc(sems["st"], 16)
         elif op[0] == "XY":
             g.dma_start(T.y[:, :], T.x[:, :]).then_inc(sems["st"], 16)
         else:
             trs = []
-            for (p, dsts, mask, sem) in op[1]:
+            for ((b, s), dsts, mask, sem) in op[1]:
                 ids = [bass.DstId(rid=topo.addr(d)[0], pnc=topo.addr(d)[1]) for d in dsts]
                 trs.append(bass.RemoteDMATransfer(dst_ids=ids, dma_engine_mask=mask, remote_sem=sems[sem],
-                                                  srcs=[T.buf[p]], dsts=[T.buf[p] for d in dsts], alu_op=0))
+                                                  srcs=[bufs[b][s]], dsts=[bufs[b][s] for d in dsts], alu_op=0))
             g.remote_dma_fused(trs, local_sem=sems["sent"])

import concourse.bass as bass
import comms_topo

FAR = 4

ROOT = 29
RANKS = [8 * ch + 2 for ch in range(16) if ch != 3]
EVEN_R = [r for r in RANKS if (r // 8) % 2 == 0]
ODD_R = [r for r in RANKS if (r // 8) % 2 == 1]
ODD = [1, 5, 7, 9, 11, 13, 15]
HELP = [30, 26, 31, 27]
SIDE = [24, 25, 24, 25]


def eng(lo, n):
    return ((1 << n) - 1) << lo


def finish(prog, groups):
    for r in RANKS:
        for j, (b, lo, hi) in enumerate(groups):
            prog[r].append(("W", "g%d" % j))
            prog[r].append(("ST", b, lo, hi))
        prog[r].append(("W", "st"))
    for c in prog:
        if any(op[0] == "S" for op in prog[c]):
            prog[c].append(("W", "sent"))
    tot = {}
    for c in prog:
        for op in prog[c]:
            if op[0] == "S":
                for (p, dsts, mask, sem) in op[1]:
                    n = bin(mask).count("1")
                    tot[(c, "sent")] = tot.get((c, "sent"), 0) + n
                    for d in dsts:
                        tot[(d, sem)] = tot.get((d, sem), 0) + n
            elif op[0] == "LD":
                tot[(c, op[4])] = tot.get((c, op[4]), 0) + 16
            elif op[0] in ("ST", "XY"):
                tot[(c, "st")] = tot.get((c, "st"), 0) + 16
    return prog, tot


def resend(core, piece, gname, far):
    if not far:
        return [(piece, [r for r in RANKS if r > core] + [r for r in RANKS if r < core], 0xFF, gname)]
    ev = [r for r in EVEN_R if r > core] + [r for r in EVEN_R if r < core]
    od = [r for r in ODD_R if r > core] + [r for r in ODD_R if r < core]
    w = 8 // far
    return [(piece, ev[s::far] + od[s::far], eng(s * w, w), gname) for s in range(far)]


def build(far):
    counts_o = [8, 8, 8, 4]
    counts = [12, 8, 8, 4]
    prog = {c: [] for c in range(128)}
    root = prog[ROOT]
    for q in range(4):
        root.append(("LD", q, 0, counts[q], "ld%d" % q))
    groups = [(0, 0, 4), (0, 4, 12), (1, 0, 8), (2, 0, 8), (3, 0, 4)]
    first = [((0, i), [HELP[i], SIDE[i]], eng(8 + 2 * i, 2), "pc") for i in range(4)]
    n = max(1, far)
    m = max(1, far // 2)
    for i in range(4):
        prog[HELP[i]].append(("W", "pc"))
        prog[HELP[i]].append(("S", [((0, i), EVEN_R[s::n], eng(s * (8 // n), 8 // n), "g0") for s in range(n)]))
    for s in range(2):
        prog[24 + s].append(("W", "pc"))
        prog[24 + s].append(("S", [((0, s + 2 * a), ODD_R[b::m], eng((a * m + b) * (4 // m), 4 // m), "g0")
                                   for a in range(2) for b in range(m)]))
    k = 0
    for q in range(4):
        base = 4 if q == 0 else 0
        wo = 8 // counts_o[q]
        trs = list(first) if q == 0 else []
        for i in range(counts_o[q]):
            core = 8 * ODD[k % 7] + [2, 6, 3, 7][k // 7]
            k += 1
            trs.append(((q, base + i), [core], eng(i * wo, wo), "pc"))
            prog[core].append(("W", "pc"))
            prog[core].append(("S", resend(core, (q, base + i), "g%d" % (q + 1), far)))
        root.append(("W", "ld%d" % q))
        root.append(("S", trs))
    root.append(("XY",))
    root.append(("W", "st"))
    return ([64, 64, 64, 64], counts) + finish(prog, groups)


NCOLS, COUNTS, PROG, TOTAL = build(FAR)
ROW0 = [0]
for q in range(4):
    ROW0.append(ROW0[q] + COUNTS[q] * NCOLS[q] // 16)

SCRATCH = {
    "bufa": ("dram", [COUNTS[0], 128, NCOLS[0]], "bfloat16"),
    "bufb": ("dram", [COUNTS[1], 128, NCOLS[1]], "bfloat16"),
    "bufc": ("dram", [COUNTS[2], 128, NCOLS[2]], "bfloat16"),
    "bufd": ("dram", [COUNTS[3], 128, NCOLS[3]], "bfloat16"),
}
SEMAPHORES = ["ld0", "ld1", "ld2", "ld3", "st", "sent", "pc", "g0", "g1", "g2", "g3", "g4"]


def rank_program(g, core, T, topo):
    sems = {"ld0": T.sem.ld0, "ld1": T.sem.ld1, "ld2": T.sem.ld2, "ld3": T.sem.ld3, "st": T.sem.st,
            "sent": T.sem.sent, "pc": T.sem.pc, "g0": T.sem.g0, "g1": T.sem.g1, "g2": T.sem.g2,
            "g3": T.sem.g3, "g4": T.sem.g4}
    bufs = [T.bufa, T.bufb, T.bufc, T.bufd]
    for op in PROG[core]:
        if op[0] == "W":
            g.wait_ge(sems[op[1]], TOTAL[(core, op[1])])
        elif op[0] in ("LD", "ST"):
            b, lo, hi = op[1], op[2], op[3]
            r0 = ROW0[b] + lo * NCOLS[b] // 16
            r1 = ROW0[b] + hi * NCOLS[b] // 16
            if op[0] == "LD":
                g.dma_start(bufs[b][lo:hi], T.x[r0:r1, :]).then_inc(sems[op[4]], 16)
            else:
                g.dma_start(T.y[r0:r1, :], bufs[b][lo:hi]).then_inc(sems["st"], 16)
        elif op[0] == "XY":
            g.dma_start(T.y[:, :], T.x[:, :]).then_inc(sems["st"], 16)
        else:
            trs = []
            for ((b, s), dsts, mask, sem) in op[1]:
                ids = [bass.DstId(rid=topo.addr(d)[0], pnc=topo.addr(d)[1]) for d in dsts]
                trs.append(bass.RemoteDMATransfer(dst_ids=ids, dma_engine_mask=mask, remote_sem=sems[sem],
                                                  srcs=[bufs[b][s]], dsts=[bufs[b][s] for d in dsts], alu_op=0))
            g.remote_dma_fused(trs, local_sem=sems["sent"])
